import numpy as np
import ml_dtypes


def mxq(x, axis, fmt="e4m3"):
    dtype, down = {"e4m3": (ml_dtypes.float8_e4m3fn, 7), "e5m2": (ml_dtypes.float8_e5m2, 14)}[fmt]
    v = np.moveaxis(np.asarray(x, np.float32).astype(ml_dtypes.bfloat16).astype(np.float64), axis, -1)
    blocks = v.reshape(v.shape[:-1] + (-1, 32))
    amax = np.abs(blocks).max(-1, keepdims=True)
    byte = np.maximum(np.where(amax > 0, np.frexp(amax)[1] - 1 + 127, 0) - down, 1)
    scale = np.exp2(byte - 127.0)
    codes = (blocks / scale).astype(np.float32).astype(dtype).astype(np.float64)
    return np.moveaxis((codes * scale).reshape(v.shape), -1, axis)


WIDE = False


def mx_kscale(k):
    if not WIDE:
        return np.ones(k)
    levels = np.array([30, -30])
    if k % 512:
        return np.exp2(np.random.permutation(np.resize(levels, k // 32))).repeat(32)
    a = np.empty((k // 512, 16))
    for p in range(k // 512):
        a[p, :8] = np.random.permutation(np.resize(levels, 8))
        for g in range(8):
            far = levels[np.abs(levels - a[p, g]) >= 10]
            a[p, g + 8] = far[np.random.randint(len(far))]
    return np.exp2(a.ravel()).repeat(32)


def f64(x):
    return np.asarray(x).astype(np.float64)


def striped(idx):
    return np.tile(idx.reshape(-1, 16).T, (8, 1)).astype(np.uint16)


def unstriped(offs):
    return offs[:16].T.reshape(-1).astype(np.int64)


K, T, E, C, N = 256, 1536, 6, 512, 1024


def by_expert(wq, xq):
    return np.concatenate([wq[e].T @ xq[:, e * C:(e + 1) * C] for e in range(E)], axis=1)


def setup_inputs():
    n = np.random.standard_normal
    s = mx_kscale(N)[:, None]
    first = np.random.permutation(np.repeat(np.arange(E), T // E))
    second = (first + 1 + np.random.permutation(np.repeat(np.arange(E - 1), -(-T // (E - 1)))[:T])) % E
    while np.bincount(second, minlength=E).max() != T // E:
        load = np.bincount(second, minlength=E); hi, lo = int(load.argmax()), int(load.argmin())
        t = np.flatnonzero((second == hi) & (first != lo))[0]; second[t] = lo
    slot_token = np.empty(E * C, np.int64); pos = np.empty((2, T), np.int64); fill = np.zeros(E, np.int64)
    place = np.stack([np.random.permutation(C) for _ in range(E)])
    for r, deal in enumerate((first, second)):
        for t in np.random.permutation(T):
            e = deal[t]; j = e * C + place[e, fill[e]]; fill[e] += 1; slot_token[j] = t; pos[r, t] = j
    g = np.random.uniform(0.2, 0.8, T)
    w_slot = np.empty(E * C); w_slot[pos[0]] = g; w_slot[pos[1]] = 1.0 - g
    return {
        "dyT": (n((N, T)) * s).astype(np.float32),
        "w": (n((E, N, K)) / np.sqrt(N) / s[None]).astype(np.float32),
        "gate": np.tile(w_slot, (N, 1)).astype(np.float32),
        "offs": striped(slot_token),
        "pos1": striped(pos[0]),
        "pos2": striped(pos[1]),
    }


def reference(dyT, w, gate, offs, pos1, pos2):
    idx = unstriped(offs)
    gq = mxq(f64(gate) * f64(dyT)[:, idx], 0, "e5m2")
    dx = by_expert(mxq(f64(w), 1, "e4m3"), gq)
    return dx[:, unstriped(pos1)] + dx[:, unstriped(pos2)]

@@ -1,0 +1,167 @@
+from contextlib import ExitStack
+
+import concourse.mybir as mybir
+
+N, K, T, E, C = 1024, 256, 1536, 6, 512
+S = E * C
+FLOPS = 2 * N * K * S
+BYTES = 4 * (N * T + E * N * K + S + K * T) + 2 * 128 * (S + 2 * T) // 16
+
+F32 = mybir.dt.float32
+BF16 = mybir.dt.bfloat16
+U32 = mybir.dt.uint32
+U16 = mybir.dt.uint16
+U8 = mybir.dt.uint8
+E4M3 = mybir.dt.float8_e4m3fn_x4
+E5M2 = mybir.dt.float8_e5m2_x4
+MULT = mybir.AluOpType.mult
+ADD = mybir.AluOpType.add
+
+P = 128
+PACK = 4
+PASSES = 2
+PAIRS = E // 2
+PAIR = 2 * C
+HALVES = K // P
+
+
+def tile_moe_bdx_lin_none_kernel(tc, dyT, w, gate, offs, pos1, pos2, out):
+    nc = tc.nc
+    with ExitStack() as ctx:
+        lists = ctx.enter_context(tc.tile_pool(name="lists", bufs=1))
+        keep = ctx.enter_context(tc.tile_pool(name="keep", bufs=1))
+        planes = ctx.enter_context(tc.tile_pool(name="planes", bufs=8))
+        gathered = ctx.enter_context(tc.tile_pool(name="gathered", bufs=2))
+        rounded = ctx.enter_context(tc.tile_pool(name="rounded", bufs=2))
+        small = ctx.enter_context(tc.tile_pool(name="small", bufs=1))
+        raws = ctx.enter_context(tc.tile_pool(name="raws", bufs=3))
+        psum = ctx.enter_context(tc.psum_pool(name="psum", bufs=8))
+
+        offs_t = lists.tile([P, S // 16], U16, name="offs_t")
+        nc.sync.dma_start(offs_t[:], offs)
+        pos1_t = lists.tile([P, T // 16], U16, name="pos1_t")
+        pos2_t = lists.tile([P, T // 16], U16, name="pos2_t")
+
+        rows = dyT.rearrange("(c p t) s -> c t p s", c=PASSES, t=PACK)
+        gate_t = [keep.tile([P, PAIR], F32, name="gate%d" % q) for q in range(PAIRS)]
+        table = {}
+        for c in range(PASSES):
+            for t in range(PACK):
+                plane = planes.tile([P, T], F32, name="plane", tag="plane")
+                nc.sync.dma_start(plane[:], rows[c, t])
+                table[c, t] = plane
+                if c == 0 and t == 0:
+                    nc.sync.dma_start(gate_t[0][:, 0:C], gate[0:P, 0:C])
+                    nc.sync.dma_start(gate_t[0][:, C:PAIR], gate[0:P, C:PAIR])
+        raw = []
+        for e in range(E):
+            r = raws.tile([P, PASSES, PACK * K], F32, name="raw", tag="raw")
+            nc.sync.dma_start(r[:], w[e].rearrange("(c p j) k -> p c (j k)", c=PASSES, j=PACK))
+            raw.append(r)
+            if e % 2 == 1 and e // 2 + 1 < PAIRS:
+                q = e // 2 + 1
+                nc.sync.dma_start(gate_t[q][:], gate[0:P, q * PAIR : (q + 1) * PAIR])
+        nc.sync.dma_start(pos1_t[:], pos1)
+        nc.sync.dma_start(pos2_t[:], pos2)
+
+        result = [keep.tile([P, S], F32, name="result%d" % h) for h in range(HALVES)]
+        w_bf = {}
+        w_codes = {}
+        w_scales = {}
+        g_codes = {}
+        g_scales = {}
+
+        def round_w(q, h):
+            tile = keep.tile([P, 2, PASSES, P, PACK], BF16, name="w_bf%d%d" % (q, h), align_bytes=64)
+            for i in range(2):
+                src = raw[2 * q + i][:].rearrange("p c (j h m) -> p h c m j", j=PACK, h=HALVES)
+                nc.scalar.copy(tile[:, i], src[:, h])
+            w_bf[q, h] = tile
+
+        def quantise_w(q, h):
+            codes = keep.tile([P, 2 * PASSES * P], U32, name="w_codes%d%d" % (q, h), align_bytes=64)
+            scales = keep.tile([P, 2 * PASSES * P], U8, name="w_scales%d%d" % (q, h), align_bytes=64)
+            nc.vector.quantize_mx(codes[:].bitcast(E4M3), scales[:], w_bf[q, h][:].rearrange("p e c m j -> p (e c m j)"))
+            w_codes[q, h] = codes
+            w_scales[q, h] = scales
+
+        def gather(q, c, g4, a, cuts):
+            for t in range(PACK):
+                at = 0
+                for n in cuts if t == 0 else (sum(cuts),):
+                    first = (q * PAIR + a + at) // 16
+                    window = table[c, t][:].indirect(offs_t[:, first : first + n // 16])
+                    nc.vector.tensor_tensor(g4[:, t, at : at + n], window, gate_t[q][:, a + at : a + at + n], MULT)
+                    at += n
+
+        def round_and_quantise_g(q, c, g4, at, a, n):
+            if n == PAIR:
+                g_bf = rounded.tile([P, n, PACK], BF16, name="g_bf", tag="g_bf", align_bytes=64)
+            else:
+                g_bf = small.tile([P, n, PACK], BF16, name="g_bf_small%d_%d" % (n, a), align_bytes=64)
+            for b in range(0, n, C):
+                d = min(b + C, n)
+                nc.scalar.copy(g_bf[:, b:d, :], g4[:, :, at + b : at + d].rearrange("p t s -> p s t"))
+            nc.vector.quantize_mx(
+                g_codes[q, c][:, a : a + n].bitcast(E5M2), g_scales[q, c][:, a : a + n], g_bf[:].rearrange("p s t -> p (s t)")
+            )
+
+        def multiply(q, h):
+            for i in range(2):
+                acc = psum.tile([P, C], F32, name="acc", tag="acc")
+                for c in range(PASSES):
+                    cols = slice((i * PASSES + c) * P, (i * PASSES + c + 1) * P)
+                    slots = slice(i * C, (i + 1) * C)
+                    nc.tensor.matmul_mx(
+                        out=acc[:],
+                        lhsT=w_codes[q, h][:, cols].bitcast(E4M3),
+                        lhsT_scale=w_scales[q, h][:, cols],
+                        rhs=g_codes[q, c][:, slots].bitcast(E5M2),
+                        rhs_scale=g_scales[q, c][:, slots],
+                        start=(c == 0),
+                        stop=(c == PASSES - 1),
+                    )
+                e = 2 * q + i
+                nc.scalar.copy(result[h][:, e * C : (e + 1) * C], acc[:])
+
+        for q in range(PAIRS):
+            for c in range(PASSES):
+                g_codes[q, c] = keep.tile([P, PAIR], U32, name="g_codes%d%d" % (q, c), align_bytes=64)
+                g_scales[q, c] = keep.tile([P, PAIR], U8, name="g_scales%d%d" % (q, c), align_bytes=64)
+                if q == PAIRS - 1 and c == PASSES - 1:
+                    pieces = [(0, (768,), (512, 256)), (768, (256,), (256,))]
+                elif q == 0 and c == 0:
+                    pieces = [(0, (512, 512), (PAIR,))]
+                else:
+                    pieces = [(0, (PAIR,), (PAIR,))]
+                for a, cuts, parts in pieces:
+                    n = sum(cuts)
+                    if n == 256:
+                        g4 = small.tile([P, PACK, n], F32, name="g4_small")
+                    else:
+                        g4 = gathered.tile([P, PACK, n], F32, name="g4", tag="g4")
+                    gather(q, c, g4, a, cuts)
+                    at = 0
+                    for m in parts:
+                        round_and_quantise_g(q, c, g4, at, a + at, m)
+                        at += m
+            for h in range(HALVES):
+                round_w(q, h)
+            quantise_w(q, 0)
+            multiply(q, 0)
+        for q in range(PAIRS):
+            quantise_w(q, 1)
+        for q in range(PAIRS):
+            multiply(q, 1)
+
+        for h in range(HALVES):
+            first = planes.tile([P, T], F32, name="first", tag="plane")
+            nc.vector.tensor_copy(first[:], result[h][:].indirect(pos1_t[:]))
+            second = planes.tile([P, T], F32, name="second", tag="plane")
+            total = planes.tile([P, T], F32, name="total", tag="plane")
+            cuts = ((0, T),) if h == 0 else ((0, 896), (896, T))
+            for a, b in cuts:
+                nc.vector.tensor_copy(second[:, a:b], result[h][:].indirect(pos2_t[:, a // 16 : b // 16]))
+                engine = nc.vector if (h, b) == (1, T) else nc.gpsimd
+                engine.tensor_tensor(total[:, a:b], first[:, a:b], second[:, a:b], ADD)
+                nc.sync.dma_start(out[h * P : (h + 1) * P, a:b], total[:, a:b])

@@ -67,7 +67,9 @@ def tile_moe_bdx_lin_none_kernel(tc, dyT, w, gate, offs, pos1, pos2, out):
         result = [keep.tile([P, S], F32, name="result%d" % h) for h in range(HALVES)]
         w_bf = {}
         w_codes = {}
-        w_scales = {}
+        for q, h in ((0, 0), (1, 0), (2, 0), (0, 1)):
+            w_codes[q, h] = keep.tile([P, 2 * PASSES * P], U32, name="w_codes%d%d" % (q, h), align_bytes=64)
+        w_scales = {h: keep.tile([P, E * PASSES * P], U8, name="w_scales%d" % h, align_bytes=64) for h in range(HALVES)}
         g_codes = {}
         g_scales = {}
 
@@ -79,43 +81,47 @@ def tile_moe_bdx_lin_none_kernel(tc, dyT, w, gate, offs, pos1, pos2, out):
             w_bf[q, h] = tile
 
         def quantise_w(q, h):
-            codes = keep.tile([P, 2 * PASSES * P], U32, name="w_codes%d%d" % (q, h), align_bytes=64)
-            scales = keep.tile([P, 2 * PASSES * P], U8, name="w_scales%d%d" % (q, h), align_bytes=64)
-            nc.vector.quantize_mx(codes[:].bitcast(E4M3), scales[:], w_bf[q, h][:].rearrange("p e c m j -> p (e c m j)"))
-            w_codes[q, h] = codes
-            w_scales[q, h] = scales
+            n = 2 * PASSES * P
+            codes = w_codes[q, h][:, :]
+            scales = w_scales[h][:, q * n : (q + 1) * n]
+            nc.vector.quantize_mx(codes.bitcast(E4M3), scales, w_bf[q, h][:].rearrange("p e c m j -> p (e c m j)"))
 
-        def gather(q, c, g4, a, cuts):
-            for t in range(PACK):
-                at = 0
-                for n in cuts if t == 0 else (sum(cuts),):
-                    first = (q * PAIR + a + at) // 16
-                    window = table[c, t][:].indirect(offs_t[:, first : first + n // 16])
-                    nc.vector.tensor_tensor(g4[:, t, at : at + n], window, gate_t[q][:, a + at : a + at + n], MULT)
-                    at += n
-
-        def round_and_quantise_g(q, c, g4, at, a, n):
-            if n == PAIR:
+        def round_g(q, c, g4, at, a, n):
+            if n == 256 and a + n == PAIR:
+                g_bf = keep.tile([P, n, PACK], BF16, name="g_bf_last", tag="tail", align_bytes=64)
+            elif n == PAIR:
                 g_bf = rounded.tile([P, n, PACK], BF16, name="g_bf", tag="g_bf", align_bytes=64)
             else:
                 g_bf = small.tile([P, n, PACK], BF16, name="g_bf_small%d_%d" % (n, a), align_bytes=64)
             for b in range(0, n, C):
                 d = min(b + C, n)
-                nc.scalar.copy(g_bf[:, b:d, :], g4[:, :, at + b : at + d].rearrange("p t s -> p s t"))
-            nc.vector.quantize_mx(
-                g_codes[q, c][:, a : a + n].bitcast(E5M2), g_scales[q, c][:, a : a + n], g_bf[:].rearrange("p s t -> p (s t)")
-            )
+                src = g4[:, :, at + b : at + d].rearrange("p t s -> p s t")
+                if n == 256 and a + n < PAIR:
+                    nc.vector.tensor_copy(g_bf[:, b:d, :], src)
+                else:
+                    nc.scalar.copy(g_bf[:, b:d, :], src)
+
+            def quantise_g():
+                nc.vector.quantize_mx(
+                    g_codes[q, c][:, a : a + n].bitcast(E5M2),
+                    g_scales[q, c][:, a : a + n],
+                    g_bf[:].rearrange("p s t -> p (s t)"),
+                )
+
+            return quantise_g
 
         def multiply(q, h):
             for i in range(2):
                 acc = psum.tile([P, C], F32, name="acc", tag="acc")
                 for c in range(PASSES):
-                    cols = slice((i * PASSES + c) * P, (i * PASSES + c + 1) * P)
+                    at = (i * PASSES + c) * P
+                    cols = slice(at, at + P)
+                    scale_cols = slice(2 * q * PASSES * P + at, 2 * q * PASSES * P + at + P)
                     slots = slice(i * C, (i + 1) * C)
                     nc.tensor.matmul_mx(
                         out=acc[:],
                         lhsT=w_codes[q, h][:, cols].bitcast(E4M3),
-                        lhsT_scale=w_scales[q, h][:, cols],
+                        lhsT_scale=w_scales[h][:, scale_cols],
                         rhs=g_codes[q, c][:, slots].bitcast(E5M2),
                         rhs_scale=g_scales[q, c][:, slots],
                         start=(c == 0),
@@ -128,30 +134,46 @@ def tile_moe_bdx_lin_none_kernel(tc, dyT, w, gate, offs, pos1, pos2, out):
             for c in range(PASSES):
                 g_codes[q, c] = keep.tile([P, PAIR], U32, name="g_codes%d%d" % (q, c), align_bytes=64)
                 g_scales[q, c] = keep.tile([P, PAIR], U8, name="g_scales%d%d" % (q, c), align_bytes=64)
-                if q == PAIRS - 1 and c == PASSES - 1:
-                    pieces = [(0, (768,), (512, 256)), (768, (256,), (256,))]
-                elif q == 0 and c == 0:
-                    pieces = [(0, (512, 512), (PAIR,))]
-                else:
-                    pieces = [(0, (PAIR,), (PAIR,))]
-                for a, cuts, parts in pieces:
-                    n = sum(cuts)
-                    if n == 256:
-                        g4 = small.tile([P, PACK, n], F32, name="g4_small")
-                    else:
-                        g4 = gathered.tile([P, PACK, n], F32, name="g4", tag="g4")
-                    gather(q, c, g4, a, cuts)
-                    at = 0
-                    for m in parts:
-                        round_and_quantise_g(q, c, g4, at, a + at, m)
-                        at += m
-            for h in range(HALVES):
-                round_w(q, h)
-            quantise_w(q, 0)
-            multiply(q, 0)
-        for q in range(PAIRS):
+
+        chunks = [(q, c, 0, PAIR, (PAIR,)) for q in range(PAIRS) for c in range(PASSES)][:-1]
+        chunks += [(PAIRS - 1, PASSES - 1, 0, C, (C,)), (PAIRS - 1, PASSES - 1, C, C, (256, 256))]
+        waiting = []
+        for number, (q, c, a, n, parts) in enumerate(chunks):
+            g4 = gathered.tile([P, PACK, n], F32, name="g4", tag="g4")
+            for t in range(PACK):
+                for b in (0, C) if number == 0 and t == 0 else (0,):
+                    m = C if number == 0 and t == 0 else n
+                    first = (q * PAIR + a + b) // 16
+                    window = table[c, t][:].indirect(offs_t[:, first : first + m // 16])
+                    nc.vector.tensor_tensor(g4[:, t, b : b + m], window, gate_t[q][:, a + b : a + b + m], MULT)
+                if t == 2:
+                    for task in waiting:
+                        task()
+                    waiting = []
+            at = 0
+            for m in parts:
+                waiting.append(round_g(q, c, g4, at, a + at, m))
+                at += m
+            if c == 1 and n == PAIR:
+                for h in range(HALVES):
+                    round_w(q, h)
+                waiting.append(lambda q=q: quantise_w(q, 0))
+                waiting.append(lambda q=q: multiply(q, 0))
+                if q == 0:
+                    waiting.append(lambda: quantise_w(0, 1))
+                    waiting.append(lambda: multiply(0, 1))
+            if c == 0 and q == PAIRS - 1:
+                for h in range(HALVES):
+                    round_w(q, h)
+                waiting.append(lambda q=q: quantise_w(q, 0))
+        for task in waiting:
+            task()
+        multiply(PAIRS - 1, 0)
+        late_codes = keep.tile([P, 2, 2 * PASSES * P], U32, name="late_codes", tag="tail", align_bytes=64)
+        for q in (1, 2):
+            w_codes[q, 1] = late_codes[:, q - 1, :]
             quantise_w(q, 1)
-        for q in range(PAIRS):
+        for q in (1, 2):
             multiply(q, 1)
 
         for h in range(HALVES):
@@ -159,9 +181,9 @@ def tile_moe_bdx_lin_none_kernel(tc, dyT, w, gate, offs, pos1, pos2, out):
             nc.vector.tensor_copy(first[:], result[h][:].indirect(pos1_t[:]))
             second = planes.tile([P, T], F32, name="second", tag="plane")
             total = planes.tile([P, T], F32, name="total", tag="plane")
-            cuts = ((0, T),) if h == 0 else ((0, 896), (896, T))
-            for a, b in cuts:
+            cuts = ((0, T, nc.gpsimd),) if h == 0 else ((0, 896, nc.gpsimd), (896, 1280, nc.vector), (1280, T, nc.vector))
+            for a, b in ((0, T),) if h == 0 else ((0, 896), (896, T)):
                 nc.vector.tensor_copy(second[:, a:b], result[h][:].indirect(pos2_t[:, a // 16 : b // 16]))
-                engine = nc.vector if (h, b) == (1, T) else nc.gpsimd
+            for a, b, engine in cuts:
                 engine.tensor_tensor(total[:, a:b], first[:, a:b], second[:, a:b], ADD)
                 nc.sync.dma_start(out[h * P : (h + 1) * P, a:b], total[:, a:b])

@@ -45,19 +45,25 @@ def tile_moe_bdx_lin_none_kernel(tc, dyT, w, gate, offs, pos1, pos2, out):
         rows = dyT.rearrange("(c p t) s -> c t p s", c=PASSES, t=PACK)
         gate_t = [keep.tile([P, PAIR], F32, name="gate%d" % q) for q in range(PAIRS)]
         table = {}
+        raw = []
+
+        def load_w(e):
+            r = raws.tile([P, PASSES, PACK * K], F32, name="raw", tag="raw")
+            nc.sync.dma_start(r[:], w[e].rearrange("(c p j) k -> p c (j k)", c=PASSES, j=PACK))
+            raw.append(r)
+
         for c in range(PASSES):
             for t in range(PACK):
                 plane = planes.tile([P, T], F32, name="plane", tag="plane")
                 nc.sync.dma_start(plane[:], rows[c, t])
                 table[c, t] = plane
+                if c == 1 and t == 1:
+                    load_w(0)
                 if c == 0 and t == 0:
                     nc.sync.dma_start(gate_t[0][:, 0:C], gate[0:P, 0:C])
                     nc.sync.dma_start(gate_t[0][:, C:PAIR], gate[0:P, C:PAIR])
-        raw = []
-        for e in range(E):
-            r = raws.tile([P, PASSES, PACK * K], F32, name="raw", tag="raw")
-            nc.sync.dma_start(r[:], w[e].rearrange("(c p j) k -> p c (j k)", c=PASSES, j=PACK))
-            raw.append(r)
+        for e in range(1, E):
+            load_w(e)
             if e % 2 == 1 and e // 2 + 1 < PAIRS:
                 q = e // 2 + 1
                 nc.sync.dma_start(gate_t[q][:], gate[0:P, q * PAIR : (q + 1) * PAIR])
@@ -76,8 +82,9 @@ def tile_moe_bdx_lin_none_kernel(tc, dyT, w, gate, offs, pos1, pos2, out):
         def round_w(q, h):
             tile = keep.tile([P, 2, PASSES, P, PACK], BF16, name="w_bf%d%d" % (q, h), align_bytes=64)
             for i in range(2):
-                src = raw[2 * q + i][:].rearrange("p c (j h m) -> p h c m j", j=PACK, h=HALVES)
-                nc.scalar.copy(tile[:, i], src[:, h])
+                for c in range(PASSES):
+                    src = raw[2 * q + i][:, c, :].rearrange("p (j h m x) -> p h m j x", j=PACK, h=HALVES, x=4)
+                    nc.scalar.copy(tile[:, i, c].rearrange("p (m x) j -> p m j x", x=4), src[:, h])
             w_bf[q, h] = tile
 
         def quantise_w(q, h):
@@ -87,19 +94,20 @@ def tile_moe_bdx_lin_none_kernel(tc, dyT, w, gate, offs, pos1, pos2, out):
             nc.vector.quantize_mx(codes.bitcast(E4M3), scales, w_bf[q, h][:].rearrange("p e c m j -> p (e c m j)"))
 
         def round_g(q, c, g4, at, a, n):
-            if n == 256 and a + n == PAIR:
+            if a + n == PAIR and n < PAIR:
                 g_bf = keep.tile([P, n, PACK], BF16, name="g_bf_last", tag="tail", align_bytes=64)
+                shares = ((0, 384, nc.vector.tensor_copy), (384, C, nc.scalar.copy))
             elif n == PAIR:
                 g_bf = rounded.tile([P, n, PACK], BF16, name="g_bf", tag="g_bf", align_bytes=64)
+                shares = ((0, C, nc.scalar.copy), (C, PAIR, nc.scalar.copy))
             else:
-                g_bf = small.tile([P, n, PACK], BF16, name="g_bf_small%d_%d" % (n, a), align_bytes=64)
-            for b in range(0, n, C):
-                d = min(b + C, n)
-                src = g4[:, :, at + b : at + d].rearrange("p t s -> p s t")
-                if n == 256 and a + n < PAIR:
-                    nc.vector.tensor_copy(g_bf[:, b:d, :], src)
-                else:
-                    nc.scalar.copy(g_bf[:, b:d, :], src)
+                g_bf = small.tile([P, n, PACK], BF16, name="g_bf_small", align_bytes=64)
+                shares = ((0, C, nc.scalar.copy),)
+            for b, d, copy in shares:
+                copy(
+                    g_bf[:, b:d, :].rearrange("p (s x) t -> p s t x", x=4),
+                    g4[:, :, at + b : at + d].rearrange("p t (s x) -> p s t x", x=4),
+                )
 
             def quantise_g():
                 nc.vector.quantize_mx(
@@ -136,7 +144,7 @@ def tile_moe_bdx_lin_none_kernel(tc, dyT, w, gate, offs, pos1, pos2, out):
                 g_scales[q, c] = keep.tile([P, PAIR], U8, name="g_scales%d%d" % (q, c), align_bytes=64)
 
         chunks = [(q, c, 0, PAIR, (PAIR,)) for q in range(PAIRS) for c in range(PASSES)][:-1]
-        chunks += [(PAIRS - 1, PASSES - 1, 0, C, (C,)), (PAIRS - 1, PASSES - 1, C, C, (256, 256))]
+        chunks += [(PAIRS - 1, PASSES - 1, 0, C, (C,)), (PAIRS - 1, PASSES - 1, C, C, (C,))]
         waiting = []
         for number, (q, c, a, n, parts) in enumerate(chunks):
             g4 = gathered.tile([P, PACK, n], F32, name="g4", tag="g4")

@@ -60,8 +60,8 @@ def tile_moe_bdx_lin_none_kernel(tc, dyT, w, gate, offs, pos1, pos2, out):
                 if c == 1 and t == 1:
                     load_w(0)
                 if c == 0 and t == 0:
-                    nc.sync.dma_start(gate_t[0][:, 0:C], gate[0:P, 0:C])
-                    nc.sync.dma_start(gate_t[0][:, C:PAIR], gate[0:P, C:PAIR])
+                    nc.sync.dma_start(gate_t[0][:, 0:384], gate[0:P, 0:384])
+                    nc.sync.dma_start(gate_t[0][:, 384:PAIR], gate[0:P, 384:PAIR])
         for e in range(1, E):
             load_w(e)
             if e % 2 == 1 and e // 2 + 1 < PAIRS:
@@ -73,7 +73,7 @@ def tile_moe_bdx_lin_none_kernel(tc, dyT, w, gate, offs, pos1, pos2, out):
         result = [keep.tile([P, S], F32, name="result%d" % h) for h in range(HALVES)]
         w_bf = {}
         w_codes = {}
-        for q, h in ((0, 0), (1, 0), (2, 0), (0, 1)):
+        for q, h in ((0, 0), (1, 0), (2, 0)):
             w_codes[q, h] = keep.tile([P, 2 * PASSES * P], U32, name="w_codes%d%d" % (q, h), align_bytes=64)
         w_scales = {h: keep.tile([P, E * PASSES * P], U8, name="w_scales%d" % h, align_bytes=64) for h in range(HALVES)}
         g_codes = {}
@@ -149,8 +149,7 @@ def tile_moe_bdx_lin_none_kernel(tc, dyT, w, gate, offs, pos1, pos2, out):
         for number, (q, c, a, n, parts) in enumerate(chunks):
             g4 = gathered.tile([P, PACK, n], F32, name="g4", tag="g4")
             for t in range(PACK):
-                for b in (0, C) if number == 0 and t == 0 else (0,):
-                    m = C if number == 0 and t == 0 else n
+                for b, m in ((0, 384), (384, 640)) if number == 0 and t == 0 else ((0, n),):
                     first = (q * PAIR + a + b) // 16
                     window = table[c, t][:].indirect(offs_t[:, first : first + m // 16])
                     nc.vector.tensor_tensor(g4[:, t, b : b + m], window, gate_t[q][:, a + b : a + b + m], MULT)
@@ -167,9 +166,6 @@ def tile_moe_bdx_lin_none_kernel(tc, dyT, w, gate, offs, pos1, pos2, out):
                     round_w(q, h)
                 waiting.append(lambda q=q: quantise_w(q, 0))
                 waiting.append(lambda q=q: multiply(q, 0))
-                if q == 0:
-                    waiting.append(lambda: quantise_w(0, 1))
-                    waiting.append(lambda: multiply(0, 1))
             if c == 0 and q == PAIRS - 1:
                 for h in range(HALVES):
                     round_w(q, h)
@@ -177,21 +173,33 @@ def tile_moe_bdx_lin_none_kernel(tc, dyT, w, gate, offs, pos1, pos2, out):
         for task in waiting:
             task()
         multiply(PAIRS - 1, 0)
-        late_codes = keep.tile([P, 2, 2 * PASSES * P], U32, name="late_codes", tag="tail", align_bytes=64)
-        for q in (1, 2):
-            w_codes[q, 1] = late_codes[:, q - 1, :]
+        late_codes = keep.tile([P, PAIRS, 2 * PASSES * P], U32, name="late_codes", tag="tail", align_bytes=64)
+        for q in range(PAIRS):
+            w_codes[q, 1] = late_codes[:, q, :]
             quantise_w(q, 1)
-        for q in (1, 2):
+        for q in range(PAIRS):
             multiply(q, 1)
 
-        for h in range(HALVES):
-            first = planes.tile([P, T], F32, name="first", tag="plane")
-            nc.vector.tensor_copy(first[:], result[h][:].indirect(pos1_t[:]))
-            second = planes.tile([P, T], F32, name="second", tag="plane")
-            total = planes.tile([P, T], F32, name="total", tag="plane")
-            cuts = ((0, T, nc.gpsimd),) if h == 0 else ((0, 896, nc.gpsimd), (896, 1280, nc.vector), (1280, T, nc.vector))
-            for a, b in ((0, T),) if h == 0 else ((0, 896), (896, T)):
-                nc.vector.tensor_copy(second[:, a:b], result[h][:].indirect(pos2_t[:, a // 16 : b // 16]))
-            for a, b, engine in cuts:
-                engine.tensor_tensor(total[:, a:b], first[:, a:b], second[:, a:b], ADD)
-                nc.sync.dma_start(out[h * P : (h + 1) * P, a:b], total[:, a:b])
+        def fetch(tile, h, pos, a, b):
+            nc.vector.tensor_copy(tile[:, a:b], result[h][:].indirect(pos[:, a // 16 : b // 16]))
+
+        def add_and_store(engine, h, first, second, a, b):
+            total = planes.tile([P, b - a], F32, name="total", tag="plane")
+            engine.tensor_tensor(total[:], first[:, a:b], second[:, a:b], ADD)
+            nc.sync.dma_start(out[h * P : (h + 1) * P, a:b], total[:])
+
+        first = planes.tile([P, T], F32, name="first", tag="plane")
+        second = planes.tile([P, T], F32, name="second", tag="plane")
+        fetch(first, 0, pos1_t, 0, T)
+        fetch(second, 0, pos2_t, 0, T)
+        add_and_store(nc.gpsimd, 0, first, second, 0, T)
+        first = planes.tile([P, T], F32, name="first", tag="plane")
+        second = planes.tile([P, T], F32, name="second", tag="plane")
+        fetch(first, 1, pos1_t, 0, 768)
+        fetch(second, 1, pos2_t, 0, 768)
+        add_and_store(nc.gpsimd, 1, first, second, 0, 768)
+        fetch(first, 1, pos1_t, 768, T)
+        fetch(second, 1, pos2_t, 768, 1152)
+        add_and_store(nc.gpsimd, 1, first, second, 768, 1152)
+        fetch(second, 1, pos2_t, 1152, T)
+        add_and_store(nc.vector, 1, first, second, 1152, T)

from contextlib import ExitStack

import concourse.mybir as mybir

N, K, T, E, C = 1024, 256, 1536, 6, 512
S = E * C
FLOPS = 2 * N * K * S
BYTES = 4 * (N * T + E * N * K + S + K * T) + 2 * 128 * (S + 2 * T) // 16

F32 = mybir.dt.float32
BF16 = mybir.dt.bfloat16
U32 = mybir.dt.uint32
U16 = mybir.dt.uint16
U8 = mybir.dt.uint8
E4M3 = mybir.dt.float8_e4m3fn_x4
E5M2 = mybir.dt.float8_e5m2_x4
MULT = mybir.AluOpType.mult
ADD = mybir.AluOpType.add

P = 128
PACK = 4
PASSES = 2
PAIRS = E // 2
PAIR = 2 * C
HALVES = K // P


def tile_moe_bdx_lin_none_kernel(tc, dyT, w, gate, offs, pos1, pos2, out):
    nc = tc.nc
    with ExitStack() as ctx:
        lists = ctx.enter_context(tc.tile_pool(name="lists", bufs=1))
        keep = ctx.enter_context(tc.tile_pool(name="keep", bufs=1))
        planes = ctx.enter_context(tc.tile_pool(name="planes", bufs=8))
        gathered = ctx.enter_context(tc.tile_pool(name="gathered", bufs=2))
        rounded = ctx.enter_context(tc.tile_pool(name="rounded", bufs=2))
        small = ctx.enter_context(tc.tile_pool(name="small", bufs=1))
        raws = ctx.enter_context(tc.tile_pool(name="raws", bufs=3))
        psum = ctx.enter_context(tc.psum_pool(name="psum", bufs=8))

        offs_t = lists.tile([P, S // 16], U16, name="offs_t")
        nc.sync.dma_start(offs_t[:], offs)
        pos1_t = lists.tile([P, T // 16], U16, name="pos1_t")
        pos2_t = lists.tile([P, T // 16], U16, name="pos2_t")

        rows = dyT.rearrange("(c p t) s -> c t p s", c=PASSES, t=PACK)
        gate_t = [keep.tile([P, PAIR], F32, name="gate%d" % q) for q in range(PAIRS)]
        table = {}
        raw = []

        def load_w(e):
            r = raws.tile([P, PASSES, PACK * K], F32, name="raw", tag="raw")
            nc.sync.dma_start(r[:], w[e].rearrange("(c p j) k -> p c (j k)", c=PASSES, j=PACK))
            raw.append(r)

        for c in range(PASSES):
            for t in range(PACK):
                plane = planes.tile([P, T], F32, name="plane", tag="plane")
                nc.sync.dma_start(plane[:], rows[c, t])
                table[c, t] = plane
                if c == 1 and t == 1:
                    load_w(0)
                if c == 0 and t == 0:
                    nc.sync.dma_start(gate_t[0][:, 0:384], gate[0:P, 0:384])
                    nc.sync.dma_start(gate_t[0][:, 384:PAIR], gate[0:P, 384:PAIR])
        for e in range(1, E):
            load_w(e)
            if e % 2 == 1 and e // 2 + 1 < PAIRS:
                q = e // 2 + 1
                nc.sync.dma_start(gate_t[q][:], gate[0:P, q * PAIR : (q + 1) * PAIR])
        nc.sync.dma_start(pos1_t[:], pos1)
        nc.sync.dma_start(pos2_t[:], pos2)

        result = [keep.tile([P, S], F32, name="result%d" % h) for h in range(HALVES)]
        w_bf = {}
        w_codes = {}
        for q, h in ((0, 0), (1, 0), (2, 0)):
            w_codes[q, h] = keep.tile([P, 2 * PASSES * P], U32, name="w_codes%d%d" % (q, h), align_bytes=64)
        w_scales = {h: keep.tile([P, E * PASSES * P], U8, name="w_scales%d" % h, align_bytes=64) for h in range(HALVES)}
        g_codes = {}
        g_scales = {}

        def round_w(q, h):
            tile = keep.tile([P, 2, PASSES, P, PACK], BF16, name="w_bf%d%d" % (q, h), align_bytes=64)
            for i in range(2):
                for c in range(PASSES):
                    src = raw[2 * q + i][:, c, :].rearrange("p (j h m x) -> p h m j x", j=PACK, h=HALVES, x=4)
                    nc.scalar.copy(tile[:, i, c].rearrange("p (m x) j -> p m j x", x=4), src[:, h])
            w_bf[q, h] = tile

        def quantise_w(q, h):
            n = 2 * PASSES * P
            codes = w_codes[q, h][:, :]
            scales = w_scales[h][:, q * n : (q + 1) * n]
            nc.vector.quantize_mx(codes.bitcast(E4M3), scales, w_bf[q, h][:].rearrange("p e c m j -> p (e c m j)"))

        def round_g(q, c, g4, at, a, n):
            if a + n == PAIR and n < PAIR:
                g_bf = keep.tile([P, n, PACK], BF16, name="g_bf_last", tag="tail", align_bytes=64)
                shares = ((0, 384, nc.vector.tensor_copy), (384, C, nc.scalar.copy))
            elif n == PAIR:
                g_bf = rounded.tile([P, n, PACK], BF16, name="g_bf", tag="g_bf", align_bytes=64)
                shares = ((0, C, nc.scalar.copy), (C, PAIR, nc.scalar.copy))
            else:
                g_bf = small.tile([P, n, PACK], BF16, name="g_bf_small", align_bytes=64)
                shares = ((0, C, nc.scalar.copy),)
            for b, d, copy in shares:
                copy(
                    g_bf[:, b:d, :].rearrange("p (s x) t -> p s t x", x=4),
                    g4[:, :, at + b : at + d].rearrange("p t (s x) -> p s t x", x=4),
                )

            def quantise_g():
                nc.vector.quantize_mx(
                    g_codes[q, c][:, a : a + n].bitcast(E5M2),
                    g_scales[q, c][:, a : a + n],
                    g_bf[:].rearrange("p s t -> p (s t)"),
                )

            return quantise_g

        def multiply(q, h):
            for i in range(2):
                acc = psum.tile([P, C], F32, name="acc", tag="acc")
                for c in range(PASSES):
                    at = (i * PASSES + c) * P
                    cols = slice(at, at + P)
                    scale_cols = slice(2 * q * PASSES * P + at, 2 * q * PASSES * P + at + P)
                    slots = slice(i * C, (i + 1) * C)
                    nc.tensor.matmul_mx(
                        out=acc[:],
                        lhsT=w_codes[q, h][:, cols].bitcast(E4M3),
                        lhsT_scale=w_scales[h][:, scale_cols],
                        rhs=g_codes[q, c][:, slots].bitcast(E5M2),
                        rhs_scale=g_scales[q, c][:, slots],
                        start=(c == 0),
                        stop=(c == PASSES - 1),
                    )
                e = 2 * q + i
                nc.scalar.copy(result[h][:, e * C : (e + 1) * C], acc[:])

        for q in range(PAIRS):
            for c in range(PASSES):
                g_codes[q, c] = keep.tile([P, PAIR], U32, name="g_codes%d%d" % (q, c), align_bytes=64)
                g_scales[q, c] = keep.tile([P, PAIR], U8, name="g_scales%d%d" % (q, c), align_bytes=64)

        chunks = [(q, c, 0, PAIR, (PAIR,)) for q in range(PAIRS) for c in range(PASSES)][:-1]
        chunks += [(PAIRS - 1, PASSES - 1, 0, C, (C,)), (PAIRS - 1, PASSES - 1, C, C, (C,))]
        waiting = []
        for number, (q, c, a, n, parts) in enumerate(chunks):
            g4 = gathered.tile([P, PACK, n], F32, name="g4", tag="g4")
            for t in range(PACK):
                for b, m in ((0, 384), (384, 640)) if number == 0 and t == 0 else ((0, n),):
                    first = (q * PAIR + a + b) // 16
                    window = table[c, t][:].indirect(offs_t[:, first : first + m // 16])
                    nc.vector.tensor_tensor(g4[:, t, b : b + m], window, gate_t[q][:, a + b : a + b + m], MULT)
                if t == 2:
                    for task in waiting:
                        task()
                    waiting = []
            at = 0
            for m in parts:
                waiting.append(round_g(q, c, g4, at, a + at, m))
                at += m
            if c == 1 and n == PAIR:
                for h in range(HALVES):
                    round_w(q, h)
                waiting.append(lambda q=q: quantise_w(q, 0))
                waiting.append(lambda q=q: multiply(q, 0))
            if c == 0 and q == PAIRS - 1:
                for h in range(HALVES):
                    round_w(q, h)
                waiting.append(lambda q=q: quantise_w(q, 0))
        for task in waiting:
            task()
        multiply(PAIRS - 1, 0)
        late_codes = keep.tile([P, PAIRS, 2 * PASSES * P], U32, name="late_codes", tag="tail", align_bytes=64)
        for q in range(PAIRS):
            w_codes[q, 1] = late_codes[:, q, :]
            quantise_w(q, 1)
        for q in range(PAIRS):
            multiply(q, 1)

        def fetch(tile, h, pos, a, b):
            nc.vector.tensor_copy(tile[:, a:b], result[h][:].indirect(pos[:, a // 16 : b // 16]))

        def add_and_store(engine, h, first, second, a, b):
            total = planes.tile([P, b - a], F32, name="total", tag="plane")
            engine.tensor_tensor(total[:], first[:, a:b], second[:, a:b], ADD)
            nc.sync.dma_start(out[h * P : (h + 1) * P, a:b], total[:])

        first = planes.tile([P, T], F32, name="first", tag="plane")
        second = planes.tile([P, T], F32, name="second", tag="plane")
        fetch(first, 0, pos1_t, 0, T)
        fetch(second, 0, pos2_t, 0, T)
        add_and_store(nc.gpsimd, 0, first, second, 0, T)
        first = planes.tile([P, T], F32, name="first", tag="plane")
        second = planes.tile([P, T], F32, name="second", tag="plane")
        fetch(first, 1, pos1_t, 0, 768)
        fetch(second, 1, pos2_t, 0, 768)
        add_and_store(nc.gpsimd, 1, first, second, 0, 768)
        fetch(first, 1, pos1_t, 768, T)
        fetch(second, 1, pos2_t, 768, 1152)
        add_and_store(nc.gpsimd, 1, first, second, 768, 1152)
        fetch(second, 1, pos2_t, 1152, T)
        add_and_store(nc.vector, 1, first, second, 1152, T)
